import numpy as np
import ml_dtypes


def mxq(x, axis, fmt="e4m3"):
    dtype, down = {"e4m3": (ml_dtypes.float8_e4m3fn, 7), "e5m2": (ml_dtypes.float8_e5m2, 14)}[fmt]
    v = np.moveaxis(np.asarray(x, np.float32).astype(ml_dtypes.bfloat16).astype(np.float64), axis, -1)
    blocks = v.reshape(v.shape[:-1] + (-1, 32))
    amax = np.abs(blocks).max(-1, keepdims=True)
    byte = np.maximum(np.where(amax > 0, np.frexp(amax)[1] - 1 + 127, 0) - down, 1)
    scale = np.exp2(byte - 127.0)
    codes = (blocks / scale).astype(np.float32).astype(dtype).astype(np.float64)
    return np.moveaxis((codes * scale).reshape(v.shape), -1, axis)


WIDE = False


def mx_kscale(k):
    if not WIDE:
        return np.ones(k)
    levels = np.array([10, -10, 5, -5, 0])
    if k % 512:
        return np.exp2(np.random.permutation(np.resize(levels, k // 32))).repeat(32)
    a = np.empty((k // 512, 16))
    for p in range(k // 512):
        a[p, :8] = np.random.permutation(np.resize(levels, 8))
        for g in range(8):
            far = levels[np.abs(levels - a[p, g]) >= 10]
            a[p, g + 8] = far[np.random.randint(len(far))]
    return np.exp2(a.ravel()).repeat(32)


BF16 = ml_dtypes.bfloat16


def bf(x):
    return np.asarray(x, np.float32).astype(BF16)


def f64(x):
    return np.asarray(x).astype(np.float64)

def planes(Y):
    n, m = Y.shape
    b = f64(bf(Y)).reshape(n // 32, 32, m)
    amax = np.abs(b).max(1)
    byte = np.clip(np.where(amax > 0, np.frexp(amax)[1] - 1 + 127 - 7, 1), 1, 254)
    codes = (b * np.exp2(127.0 - byte)[:, None, :]).reshape(n, m).astype(np.float32).astype(ml_dtypes.float8_e4m3fn).view(np.uint8)
    words = codes.reshape(n // 512, 128, 4, m).transpose(0, 1, 3, 2)
    return np.ascontiguousarray(words), np.ascontiguousarray(byte.astype(np.uint8).reshape(n // 512, 16, m))


B, N, C, E = 2, 512, 1024, 512


def setup_inputs():
    s, t = mx_kscale(N), mx_kscale(E)
    f1 = np.random.standard_normal((B, N, C))
    f2 = np.random.standard_normal((B, N, E))
    gt = np.random.standard_normal((B, C, E))
    w = np.random.uniform(0.5, 1.5, (B, N))
    lam = 1.0 + 0.1 * np.random.standard_normal(E)
    return {"f1": bf(f1), "f2": bf(f2 / s[:, None] * t[None, :]), "gt": bf(gt * t), "w": bf(w * s), "lam": bf(lam / (t * t))}


def weighted_cross_gram(f1, f2, w):
    n = f1.shape[1]
    a = f1 * w[:, :, None]
    aq = mxq(a, 1, "e4m3")
    f2q = mxq(f2, 1, "e4m3")
    return (aq.transpose(0, 2, 1) @ f2q) / np.sqrt(n)


def core(f1, f2, gt, w, lam):
    f1, f2, gt, w, lam = f64(f1), f64(f2), f64(gt), f64(w), f64(lam)
    e = f2.shape[2]
    g = weighted_cross_gram(f1, f2, w)
    delta = (g - gt) * lam[None, None, :]
    p = (mxq(f2, 2, "e4m3") @ mxq(delta, 2, "e4m3").transpose(0, 2, 1)) / np.sqrt(e)
    return w[:, :, None] * p


def reference(f1, f2, gt, w, lam):
    R_out = core(f1, f2, gt, w, lam)
    words, scales = planes(np.moveaxis(R_out, 1, 0).reshape(512, -1))
    return R_out, words, scales

@@ -1,0 +1,289 @@
+from contextlib import ExitStack
+
+import concourse.mybir as mybir
+from concourse.masks import make_identity
+
+F32 = mybir.dt.float32
+BF16 = mybir.dt.bfloat16
+U32 = mybir.dt.uint32
+I32 = mybir.dt.int32
+U8 = mybir.dt.uint8
+FP8X4 = mybir.dt.float8_e4m3fn_x4
+COPY = mybir.ActivationFunctionType.Copy
+MULT = mybir.AluOpType.mult
+ADD = mybir.AluOpType.add
+SUB = mybir.AluOpType.subtract
+
+B, N, C, E = 2, 512, 1024, 512
+P = 128
+W = 512
+INV = 1.0 / 512.0**0.5
+FLOPS = 2 * B * N * C * E * 2
+
+
+def tile_flowofsolutiongramgradient_x1_kernel(tc, f1, f2, gt, w, lam, out_0, out_1, out_2):
+    nc = tc.nc
+    with ExitStack() as ctx:
+        keep = ctx.enter_context(tc.tile_pool(name="keep", bufs=1))
+        pool = ctx.enter_context(tc.tile_pool(name="pool", bufs=2))
+        ptr = ctx.enter_context(tc.psum_pool(name="ptr", bufs=2))
+        pmx = ctx.enter_context(tc.psum_pool(name="pmx", bufs=6))
+
+        ident = keep.tile([P, P], F32, name="ident")
+        make_identity(nc, ident[:])
+        wb = keep.tile([P, B, 4], BF16, name="wb")
+        lb = keep.tile([P, 4], BF16, name="lb")
+        wf = keep.tile([P, B, 4], F32, name="wf")
+        ws = keep.tile([P, B, 4], F32, name="ws")
+        lf = keep.tile([P, 4], F32, name="lf")
+        ls = keep.tile([P, 4], F32, name="ls")
+
+        d = {}
+
+        def load(key):
+            kind, i = key
+            if kind == "f2":
+                t = pool.tile([P, 4, E], BF16, name="f2t", bufs=2)
+                nc.sync.dma_start(out=t[:], in_=f2[i].rearrange("(p j) e -> p j e", j=4))
+            elif kind == "f1":
+                b, h = divmod(i, 2)
+                t = pool.tile([P, 4, W], BF16, name="f1t", bufs=4)
+                nc.sync.dma_start(out=t[:], in_=f1[b][:, h * W : h * W + W].rearrange("(p j) c -> p j c", j=4))
+            else:
+                b, h = divmod(i, 2)
+                t = pool.tile([P, 4, E], BF16, name="gtt", bufs=4)
+                nc.sync.dma_start(out=t[:], in_=gt[b][h * W : h * W + W, :].rearrange("(p k) e -> p k e", k=4))
+            d[key] = t
+
+        def copy(eng, out, in_):
+            if eng == "V":
+                nc.vector.tensor_copy(out=out, in_=in_)
+            elif eng == "G":
+                nc.gpsimd.tensor_scalar(out=out, in0=in_, scalar1=1.0, scalar2=0.0, op0=MULT, op1=ADD)
+            else:
+                nc.scalar.copy(out=out, in_=in_)
+
+        def interleave(eng, out, in_):
+            copy(eng, out[:].rearrange("p (c i) t -> p c t i", i=4), in_[:].rearrange("p t (c i) -> p c t i", i=4))
+
+        def quant(kind, i, src, bufs):
+            codes = pool.tile([P, W], U32, name=kind + "_codes", bufs=bufs, align_bytes=64)
+            scales = pool.tile([P, W], U8, name=kind + "_scales", bufs=bufs, align_bytes=64)
+            nc.vector.quantize_mx(out=codes[:].bitcast(FP8X4), scales=scales[:], in_=src[:].rearrange("p c t -> p (c t)"))
+            d[kind, i] = (codes, scales)
+
+        def mm(out, lhs, t, rhs):
+            nc.tensor.matmul_mx(
+                out=out,
+                lhsT=lhs[0][:, t * P : t * P + P].bitcast(FP8X4),
+                lhsT_scale=lhs[1][:, t * P : t * P + P],
+                rhs=rhs[0][:].bitcast(FP8X4),
+                rhs_scale=rhs[1][:],
+                start=True,
+                stop=True,
+            )
+
+        def F1(b, e):
+            g = pool.tile([P, W, 4], BF16, name="f2g", bufs=2, align_bytes=64)
+            copy(e, g[:].rearrange("p (t m) j -> p t m j", t=4), d["f2", b][:].rearrange("p j (m t) -> p t m j", t=4))
+            d["f2g", b] = g
+
+        def F2(b, e):
+            quant("f2n", b, d["f2g", b], 2)
+
+        def T(b, e):
+            words = d["f2", b][:].bitcast(F32)
+            for jj in range(2):
+                bank = ptr.tile([P, 2, 2, P], F32, name="tr")
+                for j in range(2):
+                    for u in range(2):
+                        nc.tensor.transpose(bank[:, j, u, :], words[:, 2 * jj + j, u::2], ident[:])
+                d["T", b, jj] = bank
+
+        def F3(b, e):
+            g = pool.tile([P, W, 4], BF16, name="f2eg", bufs=2, align_bytes=64)
+            gw = g[:].rearrange("p n t -> p (n t)").bitcast(F32).rearrange("p (j m u) -> p j m u", j=4, u=2)
+            for jj in range(2):
+                copy(e, gw[:, 2 * jj : 2 * jj + 2], d["T", b, jj][:].rearrange("p j u m -> p j m u"))
+            d["f2eg", b] = g
+
+        def F4(b, e):
+            quant("f2e", b, d["f2eg", b], 2)
+
+        def A1(i, e):
+            b = i // 2
+            a = pool.tile([P, 4, W], BF16, name="anat", bufs=2)
+            for j in range(4):
+                nc.vector.tensor_scalar(out=a[:, j, :], in0=d["f1", i][:, j, :], scalar1=wf[:, b, j : j + 1], scalar2=None, op0=MULT)
+            d["anat", i] = a
+
+        def A2(i, e):
+            g = pool.tile([P, W, 4], BF16, name="agrp", bufs=2, align_bytes=64)
+            interleave(e, g, d["anat", i])
+            d["agrp", i] = g
+
+        def A3(i, e):
+            quant("a", i, d["agrp", i], 4)
+
+        def G(i, u, e):
+            words = d["gt", i][:].bitcast(F32)
+            bank = ptr.tile([P, 4, P], F32, name="tr")
+            for k in range(4):
+                nc.tensor.transpose(bank[:, k, :], words[:, k, u::2], ident[:])
+            d["G", i, u] = bank
+
+        def GL(i, u, e):
+            if ("gl", i) not in d:
+                d["gl", i] = pool.tile([P, 4, W], F32, name="gl", bufs=4)
+            halves = d["G", i, u][:].rearrange("p k m -> p (k m)").bitcast(BF16).rearrange("p (k m v) -> p m k v", k=4, v=2)
+            for v in range(2):
+                t = 2 * u + v
+                nc.scalar.activation(out=d["gl", i][:, t, :].rearrange("p (m k) -> p m k", k=4), in_=halves[:, :, :, v], func=COPY, scale=lf[:, t : t + 1])
+
+        def M1(i, h, e):
+            for t in (2 * h, 2 * h + 1):
+                bank = pmx.tile([P, W], F32, name="mx")
+                mm(bank[:], d["f2n", i // 2], t, d["a", i])
+                d["M1", i, t] = bank
+
+        def D1(i, h, e):
+            if ("dn", i) not in d:
+                d["dn", i] = pool.tile([P, 4, W], BF16, name="dn", bufs=2)
+            for t in (2 * h, 2 * h + 1):
+                nc.vector.scalar_tensor_tensor(out=d["dn", i][:, t, :], in0=d["M1", i, t][:], scalar=ls[:, t : t + 1], in1=d["gl", i][:, t, :], op0=MULT, op1=SUB)
+
+        def D2(i, e):
+            g = pool.tile([P, W, 4], BF16, name="dgrp", bufs=2, align_bytes=64)
+            interleave(e, g, d["dn", i])
+            d["dgrp", i] = g
+
+        def D3(i, e):
+            quant("delta", i, d["dgrp", i], 4)
+
+        def M2(i, h, e):
+            for t in (2 * h, 2 * h + 1):
+                bank = pmx.tile([P, W], F32, name="mx")
+                mm(bank[:], d["f2e", i // 2], t, d["delta", i])
+                d["M2", i, t] = bank
+
+        def O1(i, h, e):
+            b, c = divmod(i, 2)
+            if ("o", i) not in d:
+                d["o", i] = pool.tile([P, 4, W], F32, name="o", bufs=4)
+            o = d["o", i]
+            for t in (2 * h, 2 * h + 1):
+                if e == "V":
+                    nc.vector.tensor_scalar(out=o[:, t, :], in0=d["M2", i, t][:], scalar1=ws[:, b, t : t + 1], scalar2=None, op0=MULT)
+                else:
+                    nc.scalar.activation(out=o[:, t, :], in_=d["M2", i, t][:], func=COPY, scale=ws[:, b, t : t + 1])
+            rows = out_0[b].rearrange("(p t) c -> p t c", t=4)
+            nc.sync.dma_start(out=rows[:, 2 * h : 2 * h + 2, c * W : c * W + W], in_=o[:, 2 * h : 2 * h + 2, :])
+
+        def O2(i, e):
+            g = pool.tile([P, W, 4], BF16, name="ogrp", bufs=2, align_bytes=64)
+            interleave(e, g, d["o", i])
+            d["ogrp", i] = g
+
+        def O3(i, e):
+            quant("plane", i, d["ogrp", i], 4)
+            codes, scales = d["plane", i]
+            cols = slice(i * W, i * W + W)
+            nc.sync.dma_start(out=out_1[0][:, cols, :].rearrange("p m t -> p (m t)").bitcast(I32), in_=codes[:].bitcast(I32))
+            for q in range(4):
+                nc.sync.dma_start(out=out_2[0][4 * q : 4 * q + 4, cols].bitcast(I32), in_=scales[32 * q : 32 * q + 4, :].bitcast(I32))
+
+        with tc.manual_schedule():
+            nc.scalar.dma_start(out=wb[:], in_=w.rearrange("b (p j) -> p b j", j=4))
+            nc.scalar.dma_start(out=lb[:], in_=lam.rearrange("(p t) -> p t", t=4))
+            for key in (("f2", 0), ("f1", 0), ("gt", 0), ("f1", 1), ("gt", 1), ("f2", 1), ("f1", 2), ("gt", 2), ("f1", 3), ("gt", 3)):
+                load(key)
+            nc.scalar.activation(out=wf[:], in_=wb[:], func=COPY)
+            nc.scalar.activation(out=ws[:], in_=wb[:], func=COPY, scale=INV)
+            nc.scalar.activation(out=lf[:], in_=lb[:], func=COPY)
+            nc.scalar.activation(out=ls[:], in_=lb[:], func=COPY, scale=INV)
+            T(0, "P")
+            F1(0, "V")
+            F3(0, "S")
+            A1(0, "V")
+            F2(0, "V")
+            G(0, 0, "P")
+            A2(0, "V")
+            G(0, 1, "P")
+            GL(0, 0, "S")
+            F4(0, "V")
+            GL(0, 1, "S")
+            A3(0, "V")
+            A1(1, "V")
+            M1(0, 0, "P")
+            M1(0, 1, "P")
+            A2(1, "V")
+            G(1, 0, "P")
+            G(1, 1, "P")
+            GL(1, 0, "S")
+            D1(0, 0, "V")
+            GL(1, 1, "S")
+            A3(1, "V")
+            D1(0, 1, "V")
+            M1(1, 0, "P")
+            F1(1, "S")
+            M1(1, 1, "P")
+            A1(2, "V")
+            T(1, "P")
+            D1(1, 0, "V")
+            G(2, 0, "P")
+            D2(0, "S")
+            G(2, 1, "P")
+            A2(2, "V")
+            D1(1, 1, "V")
+            A3(2, "V")
+            F3(1, "S")
+            D3(0, "V")
+            GL(2, 0, "S")
+            D2(1, "V")
+            GL(2, 1, "S")
+            F2(1, "V")
+            M1(2, 0, "P")
+            M1(2, 1, "P")
+            D1(2, 0, "V")
+            M2(0, 0, "P")
+            M2(0, 1, "P")
+            D3(1, "V")
+            O1(0, 0, "S")
+            G(3, 0, "P")
+            D1(2, 1, "V")
+            G(3, 1, "P")
+            O1(0, 1, "S")
+            M2(1, 0, "P")
+            A1(3, "V")
+            M2(1, 1, "P")
+            GL(3, 0, "S")
+            A2(3, "V")
+            GL(3, 1, "S")
+            F4(1, "V")
+            A3(3, "V")
+            D2(2, "S")
+            O2(0, "V")
+            M1(3, 0, "P")
+            M1(3, 1, "P")
+            D1(3, 0, "V")
+            O1(1, 0, "S")
+            O3(0, "V")
+            D1(3, 1, "V")
+            O1(1, 1, "S")
+            D3(2, "V")
+            D2(3, "V")
+            M2(2, 0, "P")
+            M2(2, 1, "P")
+            O1(2, 0, "S")
+            O2(1, "V")
+            O1(2, 1, "S")
+            D3(3, "V")
+            O3(1, "V")
+            M2(3, 0, "P")
+            O2(2, "V")
+            M2(3, 1, "P")
+            O1(3, 1, "S")
+            O1(3, 0, "V")
+            O3(2, "V")
+            O2(3, "V")
+            O3(3, "V")

@@ -47,8 +47,8 @@ def tile_flowofsolutiongramgradient_x1_kernel(tc, f1, f2, gt, w, lam, out_0, out
                 nc.sync.dma_start(out=t[:], in_=f2[i].rearrange("(p j) e -> p j e", j=4))
             elif kind == "f1":
                 b, h = divmod(i, 2)
-                t = pool.tile([P, 4, W], BF16, name="f1t", bufs=4)
-                nc.sync.dma_start(out=t[:], in_=f1[b][:, h * W : h * W + W].rearrange("(p j) c -> p j c", j=4))
+                t = pool.tile([P, 2, C], BF16, name="f1t", bufs=4)
+                nc.sync.dma_start(out=t[:], in_=f1[b].rearrange("(p j) c -> p j c", j=4)[:, 2 * h : 2 * h + 2, :])
             else:
                 b, h = divmod(i, 2)
                 t = pool.tile([P, 4, E], BF16, name="gtt", bufs=4)
@@ -64,29 +64,38 @@ def tile_flowofsolutiongramgradient_x1_kernel(tc, f1, f2, gt, w, lam, out_0, out
                 nc.scalar.copy(out=out, in_=in_)
 
         def interleave(eng, out, in_):
-            copy(eng, out[:].rearrange("p (c i) t -> p c t i", i=4), in_[:].rearrange("p t (c i) -> p c t i", i=4))
+            copy(eng, out.rearrange("p (c i) t -> p c t i", i=4), in_.rearrange("p t (c i) -> p c t i", i=4))
 
-        def quant(kind, i, src, bufs):
-            codes = pool.tile([P, W], U32, name=kind + "_codes", bufs=bufs, align_bytes=64)
-            scales = pool.tile([P, W], U8, name=kind + "_scales", bufs=bufs, align_bytes=64)
-            nc.vector.quantize_mx(out=codes[:].bitcast(FP8X4), scales=scales[:], in_=src[:].rearrange("p c t -> p (c t)"))
+        def grouped(name, key, bufs):
+            if key not in d:
+                d[key] = pool.tile([P, W, 4], BF16, name=name, bufs=bufs, align_bytes=64)
+            return d[key]
+
+        def quant(kind, i, src, bufs, lo=0, n=W):
+            codes = pool.tile([P, n], U32, name=kind + "_codes", bufs=bufs, align_bytes=64)
+            scales = pool.tile([P, n], U8, name=kind + "_scales", bufs=bufs, align_bytes=64)
+            nc.vector.quantize_mx(
+                out=codes[:].bitcast(FP8X4), scales=scales[:], in_=src[:, lo : lo + n, :].rearrange("p c t -> p (c t)")
+            )
             d[kind, i] = (codes, scales)
+            return codes, scales
 
-        def mm(out, lhs, t, rhs):
+        def mm(out, lhs, t, rhs, lo=0, n=W):
             nc.tensor.matmul_mx(
                 out=out,
                 lhsT=lhs[0][:, t * P : t * P + P].bitcast(FP8X4),
                 lhsT_scale=lhs[1][:, t * P : t * P + P],
-                rhs=rhs[0][:].bitcast(FP8X4),
-                rhs_scale=rhs[1][:],
+                rhs=rhs[0][:, lo : lo + n].bitcast(FP8X4),
+                rhs_scale=rhs[1][:, lo : lo + n],
                 start=True,
                 stop=True,
             )
 
-        def F1(b, e):
-            g = pool.tile([P, W, 4], BF16, name="f2g", bufs=2, align_bytes=64)
-            copy(e, g[:].rearrange("p (t m) j -> p t m j", t=4), d["f2", b][:].rearrange("p j (m t) -> p t m j", t=4))
-            d["f2g", b] = g
+        def F1(b, e, h0, h1):
+            g = grouped("f2g", ("f2g", b), 2)
+            dst = g[:].rearrange("p (t m) j -> p t m j", t=4)
+            src = d["f2", b][:].rearrange("p j (m t) -> p t m j", t=4)
+            copy(e, dst[:, 2 * h0 : 2 * h1], src[:, 2 * h0 : 2 * h1])
 
         def F2(b, e):
             quant("f2n", b, d["f2g", b], 2)
@@ -110,17 +119,20 @@ def tile_flowofsolutiongramgradient_x1_kernel(tc, f1, f2, gt, w, lam, out_0, out
         def F4(b, e):
             quant("f2e", b, d["f2eg", b], 2)
 
-        def A1(i, e):
-            b = i // 2
-            a = pool.tile([P, 4, W], BF16, name="anat", bufs=2)
-            for j in range(4):
-                nc.vector.tensor_scalar(out=a[:, j, :], in0=d["f1", i][:, j, :], scalar1=wf[:, b, j : j + 1], scalar2=None, op0=MULT)
-            d["anat", i] = a
+        def A1(b, h, e):
+            if ("anat", b) not in d:
+                d["anat", b] = pool.tile([P, 4, C], BF16, name="anat", bufs=2)
+            for k in range(2):
+                j = 2 * h + k
+                nc.vector.tensor_scalar(
+                    out=d["anat", b][:, j, :], in0=d["f1", 2 * b + h][:, k, :], scalar1=wf[:, b, j : j + 1], scalar2=None, op0=MULT
+                )
 
-        def A2(i, e):
-            g = pool.tile([P, W, 4], BF16, name="agrp", bufs=2, align_bytes=64)
-            interleave(e, g, d["anat", i])
-            d["agrp", i] = g
+        def A2(i, e, h0, h1):
+            b, c = divmod(i, 2)
+            g = grouped("agrp", ("agrp", i), 2)
+            lo, hi = 256 * h0, 256 * h1
+            interleave(e, g[:, lo:hi, :], d["anat", b][:, :, c * W + lo : c * W + hi])
 
         def A3(i, e):
             quant("a", i, d["agrp", i], 4)
@@ -152,10 +164,10 @@ def tile_flowofsolutiongramgradient_x1_kernel(tc, f1, f2, gt, w, lam, out_0, out
             for t in (2 * h, 2 * h + 1):
                 nc.vector.scalar_tensor_tensor(out=d["dn", i][:, t, :], in0=d["M1", i, t][:], scalar=ls[:, t : t + 1], in1=d["gl", i][:, t, :], op0=MULT, op1=SUB)
 
-        def D2(i, e):
-            g = pool.tile([P, W, 4], BF16, name="dgrp", bufs=2, align_bytes=64)
-            interleave(e, g, d["dn", i])
-            d["dgrp", i] = g
+        def D2(i, e, h0, h1):
+            g = grouped("dgrp", ("dgrp", i), 2)
+            lo, hi = 256 * h0, 256 * h1
+            interleave(e, g[:, lo:hi, :], d["dn", i][:, :, lo:hi])
 
         def D3(i, e):
             quant("delta", i, d["dgrp", i], 4)
@@ -179,111 +191,146 @@ def tile_flowofsolutiongramgradient_x1_kernel(tc, f1, f2, gt, w, lam, out_0, out
             rows = out_0[b].rearrange("(p t) c -> p t c", t=4)
             nc.sync.dma_start(out=rows[:, 2 * h : 2 * h + 2, c * W : c * W + W], in_=o[:, 2 * h : 2 * h + 2, :])
 
-        def O2(i, e):
-            g = pool.tile([P, W, 4], BF16, name="ogrp", bufs=2, align_bytes=64)
-            interleave(e, g, d["o", i])
-            d["ogrp", i] = g
+        def O2(i, e, h0, h1):
+            g = grouped("ogrp", ("ogrp", i), 3)
+            lo, hi = 256 * h0, 256 * h1
+            interleave(e, g[:, lo:hi, :], d["o", i][:, :, lo:hi])
 
-        def O3(i, e):
-            quant("plane", i, d["ogrp", i], 4)
-            codes, scales = d["plane", i]
-            cols = slice(i * W, i * W + W)
+        def store_planes(i, lo, n, codes, scales):
+            cols = slice(i * W + lo, i * W + lo + n)
             nc.sync.dma_start(out=out_1[0][:, cols, :].rearrange("p m t -> p (m t)").bitcast(I32), in_=codes[:].bitcast(I32))
             for q in range(4):
                 nc.sync.dma_start(out=out_2[0][4 * q : 4 * q + 4, cols].bitcast(I32), in_=scales[32 * q : 32 * q + 4, :].bitcast(I32))
 
+        def O3(i, e):
+            codes, scales = quant("plane", i, d["ogrp", i], 3)
+            store_planes(i, 0, W, codes, scales)
+
+        def N2(i, h, e):
+            for tt in range(2):
+                bank = pmx.tile([P, 2, 256], F32, name="mx")
+                for k in range(2):
+                    mm(bank[:, k, :], d["f2e", i // 2], 2 * tt + k, d["delta", i], 256 * h, 256)
+                d["N2", i, h, tt] = bank
+
+        def Q1(i, h, e):
+            b, c = divmod(i, 2)
+            if ("o", i) not in d:
+                d["o", i] = pool.tile([P, 4, W], F32, name="o", bufs=4)
+            o = d["o", i]
+            lo = 256 * h
+            for t in range(4):
+                src = d["N2", i, h, t // 2][:, t % 2, :]
+                if e == "V":
+                    nc.vector.tensor_scalar(out=o[:, t, lo : lo + 256], in0=src, scalar1=ws[:, b, t : t + 1], scalar2=None, op0=MULT)
+                else:
+                    nc.scalar.activation(out=o[:, t, lo : lo + 256], in_=src, func=COPY, scale=ws[:, b, t : t + 1])
+            rows = out_0[b].rearrange("(p t) c -> p t c", t=4)
+            nc.sync.dma_start(out=rows[:, :, c * W + lo : c * W + lo + 256], in_=o[:, :, lo : lo + 256])
+
+        def Q3(i, h, e):
+            codes, scales = quant("half", (i, h), d["ogrp", i], 2, 256 * h, 256)
+            store_planes(i, 256 * h, 256, codes, scales)
+
         with tc.manual_schedule():
             nc.scalar.dma_start(out=wb[:], in_=w.rearrange("b (p j) -> p b j", j=4))
             nc.scalar.dma_start(out=lb[:], in_=lam.rearrange("(p t) -> p t", t=4))
-            for key in (("f2", 0), ("f1", 0), ("gt", 0), ("f1", 1), ("gt", 1), ("f2", 1), ("f1", 2), ("gt", 2), ("f1", 3), ("gt", 3)):
+            for key in (("f2", 0), ("f1", 1), ("f1", 0), ("gt", 0), ("f2", 1), ("gt", 1), ("f1", 3), ("f1", 2), ("gt", 2), ("gt", 3)):
                 load(key)
             nc.scalar.activation(out=wf[:], in_=wb[:], func=COPY)
             nc.scalar.activation(out=ws[:], in_=wb[:], func=COPY, scale=INV)
             nc.scalar.activation(out=lf[:], in_=lb[:], func=COPY)
             nc.scalar.activation(out=ls[:], in_=lb[:], func=COPY, scale=INV)
             T(0, "P")
-            F1(0, "V")
+            F1(0, "S", 1, 2)
+            F1(0, "V", 0, 1)
+            A1(0, 1, "V")
             F3(0, "S")
-            A1(0, "V")
             F2(0, "V")
-            G(0, 0, "P")
-            A2(0, "V")
+            A1(0, 0, "V")
+            A2(0, "S", 0, 2)
+            A2(1, "V", 0, 1)
             G(0, 1, "P")
-            GL(0, 0, "S")
             F4(0, "V")
+            G(0, 0, "P")
+            F1(1, "V", 0, 2)
             GL(0, 1, "S")
             A3(0, "V")
-            A1(1, "V")
-            M1(0, 0, "P")
+            F2(1, "V")
+            GL(0, 0, "S")
             M1(0, 1, "P")
-            A2(1, "V")
-            G(1, 0, "P")
+            A1(1, 1, "V")
             G(1, 1, "P")
-            GL(1, 0, "S")
-            D1(0, 0, "V")
-            GL(1, 1, "S")
-            A3(1, "V")
             D1(0, 1, "V")
-            M1(1, 0, "P")
-            F1(1, "S")
+            A2(1, "S", 1, 2)
+            M1(0, 0, "P")
+            A1(1, 0, "V")
+            GL(1, 1, "S")
+            G(1, 0, "P")
+            A3(1, "V")
+            D1(0, 0, "V")
             M1(1, 1, "P")
-            A1(2, "V")
+            GL(1, 0, "S")
+            A2(2, "V", 0, 2)
+            D2(0, "S", 1, 2)
             T(1, "P")
-            D1(1, 0, "V")
-            G(2, 0, "P")
-            D2(0, "S")
-            G(2, 1, "P")
-            A2(2, "V")
+            D2(0, "V", 0, 1)
             D1(1, 1, "V")
-            A3(2, "V")
+            M1(1, 0, "P")
             F3(1, "S")
             D3(0, "V")
+            G(2, 0, "P")
+            D1(1, 0, "V")
+            M2(0, 1, "P")
             GL(2, 0, "S")
-            D2(1, "V")
-            GL(2, 1, "S")
-            F2(1, "V")
+            A3(2, "V")
+            G(2, 1, "P")
+            A2(3, "V", 0, 2)
+            O1(0, 1, "S")
             M1(2, 0, "P")
+            GL(2, 1, "S")
+            F4(1, "V")
+            M2(0, 0, "P")
+            A3(3, "V")
+            G(3, 0, "P")
+            O1(0, 0, "S")
+            D2(1, "V", 0, 1)
             M1(2, 1, "P")
             D1(2, 0, "V")
-            M2(0, 0, "P")
-            M2(0, 1, "P")
-            D3(1, "V")
-            O1(0, 0, "S")
-            G(3, 0, "P")
-            D1(2, 1, "V")
+            D2(1, "S", 1, 2)
             G(3, 1, "P")
-            O1(0, 1, "S")
-            M2(1, 0, "P")
-            A1(3, "V")
-            M2(1, 1, "P")
-            GL(3, 0, "S")
-            A2(3, "V")
-            GL(3, 1, "S")
-            F4(1, "V")
-            A3(3, "V")
-            D2(2, "S")
-            O2(0, "V")
+            D1(2, 1, "V")
             M1(3, 0, "P")
+            GL(3, 0, "S")
+            D3(1, "V")
             M1(3, 1, "P")
+            GL(3, 1, "S")
+            D2(2, "V", 0, 1)
+            M2(1, 0, "P")
             D1(3, 0, "V")
-            O1(1, 0, "S")
-            O3(0, "V")
+            D2(2, "S", 1, 2)
             D1(3, 1, "V")
-            O1(1, 1, "S")
+            M2(1, 1, "P")
+            O1(1, 0, "S")
             D3(2, "V")
-            D2(3, "V")
-            M2(2, 0, "P")
+            O1(1, 1, "S")
+            D2(3, "V", 0, 2)
             M2(2, 1, "P")
-            O1(2, 0, "S")
-            O2(1, "V")
+            M2(2, 0, "P")
             O1(2, 1, "S")
             D3(3, "V")
+            O2(0, "V", 0, 2)
+            O1(2, 0, "S")
+            N2(3, 0, "P")
+            N2(3, 1, "P")
+            Q1(3, 0, "S")
+            O3(0, "V")
+            O2(1, "V", 0, 2)
+            Q1(3, 1, "S")
+            O2(2, "V", 0, 2)
+            O2(3, "S", 0, 1)
             O3(1, "V")
-            M2(3, 0, "P")
-            O2(2, "V")
-            M2(3, 1, "P")
-            O1(3, 1, "S")
-            O1(3, 0, "V")
+            O2(3, "S", 1, 2)
+            Q3(3, 0, "V")
             O3(2, "V")
-            O2(3, "V")
-            O3(3, "V")
+            Q3(3, 1, "V")

@@ -39,6 +39,7 @@ def tile_flowofsolutiongramgradient_x1_kernel(tc, f1, f2, gt, w, lam, out_0, out
         ls = keep.tile([P, 4], F32, name="ls")
 
         d = {}
+        left = {}
 
         def load(key):
             kind, i = key
@@ -193,18 +194,34 @@ def tile_flowofsolutiongramgradient_x1_kernel(tc, f1, f2, gt, w, lam, out_0, out
 
         def O2(i, e, h0, h1):
             g = grouped("ogrp", ("ogrp", i), 3)
-            lo, hi = 256 * h0, 256 * h1
-            interleave(e, g[:, lo:hi, :], d["o", i][:, :, lo:hi])
+            step = 128 if e == "G" else 256 * (h1 - h0)
+            for lo in range(256 * h0, 256 * h1, step):
+                interleave(e, g[:, lo : lo + step, :], d["o", i][:, :, lo : lo + step])
 
-        def store_planes(i, lo, n, codes, scales):
-            cols = slice(i * W + lo, i * W + lo + n)
+        def plane(name, i, lo, n):
+            b, c = divmod(i, 2)
+            lo_b = c * W + lo
+            if ("psc", b) not in d:
+                d["psc", b] = pool.tile([P, C], U8, name="plane_scales", bufs=2, align_bytes=64)
+                left[b] = C
+            codes = pool.tile([P, n], U32, name=name, bufs=3, align_bytes=64)
+            nc.vector.quantize_mx(
+                out=codes[:].bitcast(FP8X4),
+                scales=d["psc", b][:, lo_b : lo_b + n],
+                in_=d["ogrp", i][:, lo : lo + n, :].rearrange("p c t -> p (c t)"),
+            )
+            cols = slice(b * C + lo_b, b * C + lo_b + n)
             nc.sync.dma_start(out=out_1[0][:, cols, :].rearrange("p m t -> p (m t)").bitcast(I32), in_=codes[:].bitcast(I32))
-            for q in range(4):
-                nc.sync.dma_start(out=out_2[0][4 * q : 4 * q + 4, cols].bitcast(I32), in_=scales[32 * q : 32 * q + 4, :].bitcast(I32))
+            left[b] -= n
+            if left[b] == 0:
+                cols = slice(b * C, b * C + C)
+                for q in range(4):
+                    nc.sync.dma_start(
+                        out=out_2[0][4 * q : 4 * q + 4, cols].bitcast(I32), in_=d["psc", b][32 * q : 32 * q + 4, :].bitcast(I32)
+                    )
 
         def O3(i, e):
-            codes, scales = quant("plane", i, d["ogrp", i], 3)
-            store_planes(i, 0, W, codes, scales)
+            plane("plane_codes", i, 0, W)
 
         def N2(i, h, e):
             for tt in range(2):
@@ -229,18 +246,16 @@ def tile_flowofsolutiongramgradient_x1_kernel(tc, f1, f2, gt, w, lam, out_0, out
             nc.sync.dma_start(out=rows[:, :, c * W + lo : c * W + lo + 256], in_=o[:, :, lo : lo + 256])
 
         def Q3(i, h, e):
-            codes, scales = quant("half", (i, h), d["ogrp", i], 2, 256 * h, 256)
-            store_planes(i, 256 * h, 256, codes, scales)
+            plane("half_codes", i, 256 * h, 256)
 
         with tc.manual_schedule():
             nc.scalar.dma_start(out=wb[:], in_=w.rearrange("b (p j) -> p b j", j=4))
-            nc.scalar.dma_start(out=lb[:], in_=lam.rearrange("(p t) -> p t", t=4))
-            for key in (("f2", 0), ("f1", 1), ("f1", 0), ("gt", 0), ("f2", 1), ("gt", 1), ("f1", 3), ("f1", 2), ("gt", 2), ("gt", 3)):
+            for n, key in enumerate((("f2", 0), ("f1", 1), ("f1", 0), ("gt", 0), ("gt", 1), ("f2", 1), ("f1", 3), ("f1", 2), ("gt", 2), ("gt", 3))):
                 load(key)
-            nc.scalar.activation(out=wf[:], in_=wb[:], func=COPY)
-            nc.scalar.activation(out=ws[:], in_=wb[:], func=COPY, scale=INV)
-            nc.scalar.activation(out=lf[:], in_=lb[:], func=COPY)
-            nc.scalar.activation(out=ls[:], in_=lb[:], func=COPY, scale=INV)
+                if n == 3:
+                    nc.sync.dma_start(out=lb[:], in_=lam.rearrange("(p t) -> p t", t=4))
+            for dst, src, f in ((wf, wb, 1.0), (ws, wb, INV), (lf, lb, 1.0), (ls, lb, INV)):
+                nc.gpsimd.tensor_scalar(out=dst[:], in0=src[:], scalar1=f, scalar2=0.0, op0=MULT, op1=ADD)
             T(0, "P")
             F1(0, "S", 1, 2)
             F1(0, "V", 0, 1)
@@ -248,89 +263,90 @@ def tile_flowofsolutiongramgradient_x1_kernel(tc, f1, f2, gt, w, lam, out_0, out
             F3(0, "S")
             F2(0, "V")
             A1(0, 0, "V")
-            A2(0, "S", 0, 2)
-            A2(1, "V", 0, 1)
+            A2(1, "S", 0, 2)
+            A2(0, "V", 0, 2)
             G(0, 1, "P")
-            F4(0, "V")
             G(0, 0, "P")
-            F1(1, "V", 0, 2)
-            GL(0, 1, "S")
+            F4(0, "V")
             A3(0, "V")
-            F2(1, "V")
-            GL(0, 0, "S")
-            M1(0, 1, "P")
-            A1(1, 1, "V")
-            G(1, 1, "P")
-            D1(0, 1, "V")
-            A2(1, "S", 1, 2)
-            M1(0, 0, "P")
-            A1(1, 0, "V")
-            GL(1, 1, "S")
-            G(1, 0, "P")
+            GL(0, 1, "S")
             A3(1, "V")
-            D1(0, 0, "V")
-            M1(1, 1, "P")
+            M1(0, 0, "P")
+            F1(1, "V", 0, 2)
+            GL(0, 0, "S")
+            G(1, 0, "P")
+            A1(1, 1, "V")
             GL(1, 0, "S")
-            A2(2, "V", 0, 2)
-            D2(0, "S", 1, 2)
-            T(1, "P")
-            D2(0, "V", 0, 1)
-            D1(1, 1, "V")
+            G(1, 1, "P")
+            D1(0, 0, "V")
+            M1(0, 1, "P")
+            GL(1, 1, "S")
+            A1(1, 0, "V")
             M1(1, 0, "P")
+            D1(0, 1, "V")
+            A2(2, "S", 1, 2)
+            T(1, "P")
+            F2(1, "V")
+            D2(0, "S", 1, 2)
+            A2(2, "V", 0, 1)
+            M1(1, 1, "P")
+            D2(0, "V", 0, 1)
             F3(1, "S")
-            D3(0, "V")
-            G(2, 0, "P")
-            D1(1, 0, "V")
-            M2(0, 1, "P")
-            GL(2, 0, "S")
             A3(2, "V")
+            D3(0, "V")
+            A2(3, "S", 1, 2)
+            G(2, 0, "P")
+            A2(3, "V", 0, 1)
+            M2(0, 1, "P")
+            D1(1, 0, "V")
+            GL(2, 0, "S")
             G(2, 1, "P")
-            A2(3, "V", 0, 2)
+            D1(1, 1, "V")
             O1(0, 1, "S")
-            M1(2, 0, "P")
-            GL(2, 1, "S")
-            F4(1, "V")
-            M2(0, 0, "P")
-            A3(3, "V")
-            G(3, 0, "P")
-            O1(0, 0, "S")
-            D2(1, "V", 0, 1)
             M1(2, 1, "P")
-            D1(2, 0, "V")
+            A3(3, "V")
+            M2(0, 0, "P")
+            GL(2, 1, "S")
+            D2(1, "V", 0, 1)
+            M1(2, 0, "P")
+            F4(1, "V")
+            O1(0, 0, "S")
+            D1(2, 1, "V")
+            G(3, 0, "P")
             D2(1, "S", 1, 2)
             G(3, 1, "P")
-            D1(2, 1, "V")
+            D1(2, 0, "V")
             M1(3, 0, "P")
             GL(3, 0, "S")
             D3(1, "V")
             M1(3, 1, "P")
-            GL(3, 1, "S")
             D2(2, "V", 0, 1)
-            M2(1, 0, "P")
+            GL(3, 1, "S")
             D1(3, 0, "V")
+            M2(1, 1, "P")
             D2(2, "S", 1, 2)
             D1(3, 1, "V")
-            M2(1, 1, "P")
-            O1(1, 0, "S")
-            D3(2, "V")
+            M2(1, 0, "P")
             O1(1, 1, "S")
+            D3(2, "V")
             D2(3, "V", 0, 2)
             M2(2, 1, "P")
+            O1(1, 0, "S")
             M2(2, 0, "P")
             O1(2, 1, "S")
             D3(3, "V")
             O2(0, "V", 0, 2)
+            N2(3, 1, "P")
             O1(2, 0, "S")
             N2(3, 0, "P")
-            N2(3, 1, "P")
-            Q1(3, 0, "S")
             O3(0, "V")
-            O2(1, "V", 0, 2)
             Q1(3, 1, "S")
+            O2(1, "V", 0, 2)
+            Q1(3, 0, "S")
             O2(2, "V", 0, 2)
-            O2(3, "S", 0, 1)
-            O3(1, "V")
             O2(3, "S", 1, 2)
-            Q3(3, 0, "V")
+            O3(1, "V")
             O3(2, "V")
+            O2(3, "S", 0, 1)
             Q3(3, 1, "V")
+            Q3(3, 0, "V")

from contextlib import ExitStack

import concourse.mybir as mybir
from concourse.masks import make_identity

F32 = mybir.dt.float32
BF16 = mybir.dt.bfloat16
U32 = mybir.dt.uint32
I32 = mybir.dt.int32
U8 = mybir.dt.uint8
FP8X4 = mybir.dt.float8_e4m3fn_x4
COPY = mybir.ActivationFunctionType.Copy
MULT = mybir.AluOpType.mult
ADD = mybir.AluOpType.add
SUB = mybir.AluOpType.subtract

B, N, C, E = 2, 512, 1024, 512
P = 128
W = 512
INV = 1.0 / 512.0**0.5
FLOPS = 2 * B * N * C * E * 2


def tile_flowofsolutiongramgradient_x1_kernel(tc, f1, f2, gt, w, lam, out_0, out_1, out_2):
    nc = tc.nc
    with ExitStack() as ctx:
        keep = ctx.enter_context(tc.tile_pool(name="keep", bufs=1))
        pool = ctx.enter_context(tc.tile_pool(name="pool", bufs=2))
        ptr = ctx.enter_context(tc.psum_pool(name="ptr", bufs=2))
        pmx = ctx.enter_context(tc.psum_pool(name="pmx", bufs=6))

        ident = keep.tile([P, P], F32, name="ident")
        make_identity(nc, ident[:])
        wb = keep.tile([P, B, 4], BF16, name="wb")
        lb = keep.tile([P, 4], BF16, name="lb")
        wf = keep.tile([P, B, 4], F32, name="wf")
        ws = keep.tile([P, B, 4], F32, name="ws")
        lf = keep.tile([P, 4], F32, name="lf")
        ls = keep.tile([P, 4], F32, name="ls")

        d = {}
        left = {}

        def load(key):
            kind, i = key
            if kind == "f2":
                t = pool.tile([P, 4, E], BF16, name="f2t", bufs=2)
                nc.sync.dma_start(out=t[:], in_=f2[i].rearrange("(p j) e -> p j e", j=4))
            elif kind == "f1":
                b, h = divmod(i, 2)
                t = pool.tile([P, 2, C], BF16, name="f1t", bufs=4)
                nc.sync.dma_start(out=t[:], in_=f1[b].rearrange("(p j) c -> p j c", j=4)[:, 2 * h : 2 * h + 2, :])
            else:
                b, h = divmod(i, 2)
                t = pool.tile([P, 4, E], BF16, name="gtt", bufs=4)
                nc.sync.dma_start(out=t[:], in_=gt[b][h * W : h * W + W, :].rearrange("(p k) e -> p k e", k=4))
            d[key] = t

        def copy(eng, out, in_):
            if eng == "V":
                nc.vector.tensor_copy(out=out, in_=in_)
            elif eng == "G":
                nc.gpsimd.tensor_scalar(out=out, in0=in_, scalar1=1.0, scalar2=0.0, op0=MULT, op1=ADD)
            else:
                nc.scalar.copy(out=out, in_=in_)

        def interleave(eng, out, in_):
            copy(eng, out.rearrange("p (c i) t -> p c t i", i=4), in_.rearrange("p t (c i) -> p c t i", i=4))

        def grouped(name, key, bufs):
            if key not in d:
                d[key] = pool.tile([P, W, 4], BF16, name=name, bufs=bufs, align_bytes=64)
            return d[key]

        def quant(kind, i, src, bufs, lo=0, n=W):
            codes = pool.tile([P, n], U32, name=kind + "_codes", bufs=bufs, align_bytes=64)
            scales = pool.tile([P, n], U8, name=kind + "_scales", bufs=bufs, align_bytes=64)
            nc.vector.quantize_mx(
                out=codes[:].bitcast(FP8X4), scales=scales[:], in_=src[:, lo : lo + n, :].rearrange("p c t -> p (c t)")
            )
            d[kind, i] = (codes, scales)
            return codes, scales

        def mm(out, lhs, t, rhs, lo=0, n=W):
            nc.tensor.matmul_mx(
                out=out,
                lhsT=lhs[0][:, t * P : t * P + P].bitcast(FP8X4),
                lhsT_scale=lhs[1][:, t * P : t * P + P],
                rhs=rhs[0][:, lo : lo + n].bitcast(FP8X4),
                rhs_scale=rhs[1][:, lo : lo + n],
                start=True,
                stop=True,
            )

        def F1(b, e, h0, h1):
            g = grouped("f2g", ("f2g", b), 2)
            dst = g[:].rearrange("p (t m) j -> p t m j", t=4)
            src = d["f2", b][:].rearrange("p j (m t) -> p t m j", t=4)
            copy(e, dst[:, 2 * h0 : 2 * h1], src[:, 2 * h0 : 2 * h1])

        def F2(b, e):
            quant("f2n", b, d["f2g", b], 2)

        def T(b, e):
            words = d["f2", b][:].bitcast(F32)
            for jj in range(2):
                bank = ptr.tile([P, 2, 2, P], F32, name="tr")
                for j in range(2):
                    for u in range(2):
                        nc.tensor.transpose(bank[:, j, u, :], words[:, 2 * jj + j, u::2], ident[:])
                d["T", b, jj] = bank

        def F3(b, e):
            g = pool.tile([P, W, 4], BF16, name="f2eg", bufs=2, align_bytes=64)
            gw = g[:].rearrange("p n t -> p (n t)").bitcast(F32).rearrange("p (j m u) -> p j m u", j=4, u=2)
            for jj in range(2):
                copy(e, gw[:, 2 * jj : 2 * jj + 2], d["T", b, jj][:].rearrange("p j u m -> p j m u"))
            d["f2eg", b] = g

        def F4(b, e):
            quant("f2e", b, d["f2eg", b], 2)

        def A1(b, h, e):
            if ("anat", b) not in d:
                d["anat", b] = pool.tile([P, 4, C], BF16, name="anat", bufs=2)
            for k in range(2):
                j = 2 * h + k
                nc.vector.tensor_scalar(
                    out=d["anat", b][:, j, :], in0=d["f1", 2 * b + h][:, k, :], scalar1=wf[:, b, j : j + 1], scalar2=None, op0=MULT
                )

        def A2(i, e, h0, h1):
            b, c = divmod(i, 2)
            g = grouped("agrp", ("agrp", i), 2)
            lo, hi = 256 * h0, 256 * h1
            interleave(e, g[:, lo:hi, :], d["anat", b][:, :, c * W + lo : c * W + hi])

        def A3(i, e):
            quant("a", i, d["agrp", i], 4)

        def G(i, u, e):
            words = d["gt", i][:].bitcast(F32)
            bank = ptr.tile([P, 4, P], F32, name="tr")
            for k in range(4):
                nc.tensor.transpose(bank[:, k, :], words[:, k, u::2], ident[:])
            d["G", i, u] = bank

        def GL(i, u, e):
            if ("gl", i) not in d:
                d["gl", i] = pool.tile([P, 4, W], F32, name="gl", bufs=4)
            halves = d["G", i, u][:].rearrange("p k m -> p (k m)").bitcast(BF16).rearrange("p (k m v) -> p m k v", k=4, v=2)
            for v in range(2):
                t = 2 * u + v
                nc.scalar.activation(out=d["gl", i][:, t, :].rearrange("p (m k) -> p m k", k=4), in_=halves[:, :, :, v], func=COPY, scale=lf[:, t : t + 1])

        def M1(i, h, e):
            for t in (2 * h, 2 * h + 1):
                bank = pmx.tile([P, W], F32, name="mx")
                mm(bank[:], d["f2n", i // 2], t, d["a", i])
                d["M1", i, t] = bank

        def D1(i, h, e):
            if ("dn", i) not in d:
                d["dn", i] = pool.tile([P, 4, W], BF16, name="dn", bufs=2)
            for t in (2 * h, 2 * h + 1):
                nc.vector.scalar_tensor_tensor(out=d["dn", i][:, t, :], in0=d["M1", i, t][:], scalar=ls[:, t : t + 1], in1=d["gl", i][:, t, :], op0=MULT, op1=SUB)

        def D2(i, e, h0, h1):
            g = grouped("dgrp", ("dgrp", i), 2)
            lo, hi = 256 * h0, 256 * h1
            interleave(e, g[:, lo:hi, :], d["dn", i][:, :, lo:hi])

        def D3(i, e):
            quant("delta", i, d["dgrp", i], 4)

        def M2(i, h, e):
            for t in (2 * h, 2 * h + 1):
                bank = pmx.tile([P, W], F32, name="mx")
                mm(bank[:], d["f2e", i // 2], t, d["delta", i])
                d["M2", i, t] = bank

        def O1(i, h, e):
            b, c = divmod(i, 2)
            if ("o", i) not in d:
                d["o", i] = pool.tile([P, 4, W], F32, name="o", bufs=4)
            o = d["o", i]
            for t in (2 * h, 2 * h + 1):
                if e == "V":
                    nc.vector.tensor_scalar(out=o[:, t, :], in0=d["M2", i, t][:], scalar1=ws[:, b, t : t + 1], scalar2=None, op0=MULT)
                else:
                    nc.scalar.activation(out=o[:, t, :], in_=d["M2", i, t][:], func=COPY, scale=ws[:, b, t : t + 1])
            rows = out_0[b].rearrange("(p t) c -> p t c", t=4)
            nc.sync.dma_start(out=rows[:, 2 * h : 2 * h + 2, c * W : c * W + W], in_=o[:, 2 * h : 2 * h + 2, :])

        def O2(i, e, h0, h1):
            g = grouped("ogrp", ("ogrp", i), 3)
            step = 128 if e == "G" else 256 * (h1 - h0)
            for lo in range(256 * h0, 256 * h1, step):
                interleave(e, g[:, lo : lo + step, :], d["o", i][:, :, lo : lo + step])

        def plane(name, i, lo, n):
            b, c = divmod(i, 2)
            lo_b = c * W + lo
            if ("psc", b) not in d:
                d["psc", b] = pool.tile([P, C], U8, name="plane_scales", bufs=2, align_bytes=64)
                left[b] = C
            codes = pool.tile([P, n], U32, name=name, bufs=3, align_bytes=64)
            nc.vector.quantize_mx(
                out=codes[:].bitcast(FP8X4),
                scales=d["psc", b][:, lo_b : lo_b + n],
                in_=d["ogrp", i][:, lo : lo + n, :].rearrange("p c t -> p (c t)"),
            )
            cols = slice(b * C + lo_b, b * C + lo_b + n)
            nc.sync.dma_start(out=out_1[0][:, cols, :].rearrange("p m t -> p (m t)").bitcast(I32), in_=codes[:].bitcast(I32))
            left[b] -= n
            if left[b] == 0:
                cols = slice(b * C, b * C + C)
                for q in range(4):
                    nc.sync.dma_start(
                        out=out_2[0][4 * q : 4 * q + 4, cols].bitcast(I32), in_=d["psc", b][32 * q : 32 * q + 4, :].bitcast(I32)
                    )

        def O3(i, e):
            plane("plane_codes", i, 0, W)

        def N2(i, h, e):
            for tt in range(2):
                bank = pmx.tile([P, 2, 256], F32, name="mx")
                for k in range(2):
                    mm(bank[:, k, :], d["f2e", i // 2], 2 * tt + k, d["delta", i], 256 * h, 256)
                d["N2", i, h, tt] = bank

        def Q1(i, h, e):
            b, c = divmod(i, 2)
            if ("o", i) not in d:
                d["o", i] = pool.tile([P, 4, W], F32, name="o", bufs=4)
            o = d["o", i]
            lo = 256 * h
            for t in range(4):
                src = d["N2", i, h, t // 2][:, t % 2, :]
                if e == "V":
                    nc.vector.tensor_scalar(out=o[:, t, lo : lo + 256], in0=src, scalar1=ws[:, b, t : t + 1], scalar2=None, op0=MULT)
                else:
                    nc.scalar.activation(out=o[:, t, lo : lo + 256], in_=src, func=COPY, scale=ws[:, b, t : t + 1])
            rows = out_0[b].rearrange("(p t) c -> p t c", t=4)
            nc.sync.dma_start(out=rows[:, :, c * W + lo : c * W + lo + 256], in_=o[:, :, lo : lo + 256])

        def Q3(i, h, e):
            plane("half_codes", i, 256 * h, 256)

        with tc.manual_schedule():
            nc.scalar.dma_start(out=wb[:], in_=w.rearrange("b (p j) -> p b j", j=4))
            for n, key in enumerate((("f2", 0), ("f1", 1), ("f1", 0), ("gt", 0), ("gt", 1), ("f2", 1), ("f1", 3), ("f1", 2), ("gt", 2), ("gt", 3))):
                load(key)
                if n == 3:
                    nc.sync.dma_start(out=lb[:], in_=lam.rearrange("(p t) -> p t", t=4))
            for dst, src, f in ((wf, wb, 1.0), (ws, wb, INV), (lf, lb, 1.0), (ls, lb, INV)):
                nc.gpsimd.tensor_scalar(out=dst[:], in0=src[:], scalar1=f, scalar2=0.0, op0=MULT, op1=ADD)
            T(0, "P")
            F1(0, "S", 1, 2)
            F1(0, "V", 0, 1)
            A1(0, 1, "V")
            F3(0, "S")
            F2(0, "V")
            A1(0, 0, "V")
            A2(1, "S", 0, 2)
            A2(0, "V", 0, 2)
            G(0, 1, "P")
            G(0, 0, "P")
            F4(0, "V")
            A3(0, "V")
            GL(0, 1, "S")
            A3(1, "V")
            M1(0, 0, "P")
            F1(1, "V", 0, 2)
            GL(0, 0, "S")
            G(1, 0, "P")
            A1(1, 1, "V")
            GL(1, 0, "S")
            G(1, 1, "P")
            D1(0, 0, "V")
            M1(0, 1, "P")
            GL(1, 1, "S")
            A1(1, 0, "V")
            M1(1, 0, "P")
            D1(0, 1, "V")
            A2(2, "S", 1, 2)
            T(1, "P")
            F2(1, "V")
            D2(0, "S", 1, 2)
            A2(2, "V", 0, 1)
            M1(1, 1, "P")
            D2(0, "V", 0, 1)
            F3(1, "S")
            A3(2, "V")
            D3(0, "V")
            A2(3, "S", 1, 2)
            G(2, 0, "P")
            A2(3, "V", 0, 1)
            M2(0, 1, "P")
            D1(1, 0, "V")
            GL(2, 0, "S")
            G(2, 1, "P")
            D1(1, 1, "V")
            O1(0, 1, "S")
            M1(2, 1, "P")
            A3(3, "V")
            M2(0, 0, "P")
            GL(2, 1, "S")
            D2(1, "V", 0, 1)
            M1(2, 0, "P")
            F4(1, "V")
            O1(0, 0, "S")
            D1(2, 1, "V")
            G(3, 0, "P")
            D2(1, "S", 1, 2)
            G(3, 1, "P")
            D1(2, 0, "V")
            M1(3, 0, "P")
            GL(3, 0, "S")
            D3(1, "V")
            M1(3, 1, "P")
            D2(2, "V", 0, 1)
            GL(3, 1, "S")
            D1(3, 0, "V")
            M2(1, 1, "P")
            D2(2, "S", 1, 2)
            D1(3, 1, "V")
            M2(1, 0, "P")
            O1(1, 1, "S")
            D3(2, "V")
            D2(3, "V", 0, 2)
            M2(2, 1, "P")
            O1(1, 0, "S")
            M2(2, 0, "P")
            O1(2, 1, "S")
            D3(3, "V")
            O2(0, "V", 0, 2)
            N2(3, 1, "P")
            O1(2, 0, "S")
            N2(3, 0, "P")
            O3(0, "V")
            Q1(3, 1, "S")
            O2(1, "V", 0, 2)
            Q1(3, 0, "S")
            O2(2, "V", 0, 2)
            O2(3, "S", 1, 2)
            O3(1, "V")
            O3(2, "V")
            O2(3, "S", 0, 1)
            Q3(3, 1, "V")
            Q3(3, 0, "V")
